import numpy as np
import ml_dtypes


def mxq(x, axis, fmt="e4m3"):
    dtype, down = {"e4m3": (ml_dtypes.float8_e4m3fn, 7), "e5m2": (ml_dtypes.float8_e5m2, 14)}[fmt]
    v = np.moveaxis(np.asarray(x, np.float32).astype(ml_dtypes.bfloat16).astype(np.float64), axis, -1)
    blocks = v.reshape(v.shape[:-1] + (-1, 32))
    amax = np.abs(blocks).max(-1, keepdims=True)
    byte = np.maximum(np.where(amax > 0, np.frexp(amax)[1] - 1 + 127, 0) - down, 1)
    scale = np.exp2(byte - 127.0)
    codes = (blocks / scale).astype(np.float32).astype(dtype).astype(np.float64)
    return np.moveaxis((codes * scale).reshape(v.shape), -1, axis)


WIDE = False


def mx_kscale(k):
    if not WIDE:
        return np.ones(k)
    levels = np.array([10, -10, 5, -5, 0])
    if k % 512:
        return np.exp2(np.random.permutation(np.resize(levels, k // 32))).repeat(32)
    a = np.empty((k // 512, 16))
    for p in range(k // 512):
        a[p, :8] = np.random.permutation(np.resize(levels, 8))
        for g in range(8):
            far = levels[np.abs(levels - a[p, g]) >= 10]
            a[p, g + 8] = far[np.random.randint(len(far))]
    return np.exp2(a.ravel()).repeat(32)


def f64(x):
    return np.asarray(x).astype(np.float64)


def striped(idx):
    return np.tile(idx.reshape(-1, 16).T, (8, 1)).astype(np.uint16)


def unstriped(offs):
    return offs[:16].T.reshape(-1).astype(np.int64)


E2M1 = np.array([0.0, 0.5, 1.0, 1.5, 2.0, 3.0, 4.0, 6.0, -0.0, -0.5, -1.0, -1.5, -2.0, -3.0, -4.0, -6.0])


def pack_weight(w, fmt):
    k, n = w.shape
    w = f64(np.asarray(w, np.float32).astype(ml_dtypes.bfloat16)).reshape(k // 32, 32, n)
    amax = np.abs(w).max(1)
    if fmt == "e4m3":
        byte = np.frexp(amax)[1] - 1 + 127 - 7
    else:
        mant, ex = np.frexp(amax / 6.0)
        byte = np.where(mant > 0.5, ex, ex - 1) + 127
    byte = np.clip(np.where(amax > 0, byte, 1), 1, 254)
    scaled = (w * np.exp2(127.0 - byte)[:, None, :]).reshape(k, n).astype(np.float32)
    by_word = np.ascontiguousarray(scaled.reshape(k // 512, 128, 4, n).transpose(0, 1, 3, 2))
    if fmt == "e4m3":
        words = by_word.astype(ml_dtypes.float8_e4m3fn).view(np.uint8)
    else:
        c = by_word.astype(ml_dtypes.float4_e2m1fn).view(np.uint8) & 0xF
        words = (c[..., 0::2] | (c[..., 1::2] << 4)).reshape(k // 512, 128, 2 * n)
    return np.ascontiguousarray(words), np.ascontiguousarray(byte.astype(np.uint8).reshape(k // 512, 16, n))


def unpack_weight(words, scales, fmt):
    g, _, n = scales.shape
    words = np.ascontiguousarray(words).reshape(g, 128, n, -1)
    if fmt == "e4m3":
        vals = words.view(ml_dtypes.float8_e4m3fn).astype(np.float64)
    else:
        nib = np.empty((g, 128, n, 4), np.uint8)
        nib[..., 0::2] = words & 0xF
        nib[..., 1::2] = words >> 4
        vals = E2M1[nib]
    vals = vals * np.repeat(np.exp2(scales.astype(np.float64) - 127.0), 8, axis=1)[..., None]
    return vals.transpose(0, 1, 3, 2).reshape(g * 512, n)


def gelu(v):
    return 0.5 * v * (1.0 + np.tanh(np.sqrt(2.0 / np.pi) * (v + 0.044715 * v**3)))


K, H, T, S, T3, S2 = 1024, 1024, 2048, 512, 2048, 512


def setup_inputs():
    n = np.random.standard_normal
    s = mx_kscale(K)[:, None]
    u = mx_kscale(H)[:, None]
    tab_words, tab_scales = pack_weight(n((K, T)) * s, "e4m3")
    tab2_words, tab2_scales = pack_weight(n((H, T3)) / np.sqrt(H) / u, "e4m3")
    tab3_words, tab3_scales = pack_weight(n((H, T3)) / np.sqrt(H) / u, "e4m3")
    w2_words, w2_scales = pack_weight(n((K, H)) / np.sqrt(K) / s, "e2m1")
    return {
        "tab_words": tab_words, "tab_scales": tab_scales,
        "tab2_words": tab2_words, "tab2_scales": tab2_scales,
        "tab3_words": tab3_words, "tab3_scales": tab3_scales,
        "offs": striped(np.random.permutation(T)[:S]),
        "offs2": striped(np.random.permutation(T3)[:S2]),
        "offs3": striped(np.random.permutation(T3)[:S2]),
        "w1": (n((K, H)) / np.sqrt(K) / s).astype(np.float32),
        "w2_words": w2_words, "w2_scales": w2_scales,
        "w3": (1.5 * n((K, H)) / np.sqrt(K) / s).astype(np.float32),
        "gain": (np.exp(0.3 * n(H)) * u[:, 0]).astype(np.float32),
        "avail": np.random.uniform(0.25, 1.5, (S2, S)).astype(np.float32),
    }


def reference(tab_words, tab_scales, tab2_words, tab2_scales, tab3_words, tab3_scales,
              offs, offs2, offs3, w1, w2_words, w2_scales, w3, gain, avail):
    v = unpack_weight(tab_words, tab_scales, "e4m3")[:, unstriped(offs)]
    v2 = unpack_weight(tab2_words, tab2_scales, "e4m3")[:, unstriped(offs2)]
    v3 = unpack_weight(tab3_words, tab3_scales, "e4m3")[:, unstriped(offs3)]
    w2 = unpack_weight(w2_words, w2_scales, "e2m1")
    d1 = mxq(f64(w1), 0, "e4m3").T @ v
    d2 = w2.T @ v
    d3 = mxq(f64(w3), 0, "e4m3").T @ v
    h = f64(gain)[:, None] * (np.maximum(d1, d2) + np.tanh(d3))
    hq = mxq(h, 0, "e4m3")
    e2 = v2.T @ hq
    e3 = v3.T @ hq
    return f64(avail) * np.maximum(e2, e3)

@@ -1,0 +1,272 @@
+from contextlib import ExitStack
+
+import concourse.mybir as mybir
+from concourse.masks import make_identity
+
+K, H, T, S = 1024, 1024, 2048, 512
+FLOPS = 2 * K * H * S * 3 + 2 * H * S * S * 2
+
+F32 = mybir.dt.float32
+BF16 = mybir.dt.bfloat16
+I32 = mybir.dt.int32
+U32 = mybir.dt.uint32
+U16 = mybir.dt.uint16
+U8 = mybir.dt.uint8
+FP8X4 = mybir.dt.float8_e4m3fn_x4
+FP4X4 = mybir.dt.float4_e2m1fn_x4
+ACT = mybir.ActivationFunctionType
+ALU = mybir.AluOpType
+
+P = 128
+PACK = 4
+KP = P * PACK
+PASSES = 2
+TILES = S // P
+SCALAR_COLS = 368
+SCALAR_COLS_LAST = 176
+
+
+def tile_list_staffing_team_scores_kernel(
+    tc, tab_words, tab_scales, tab2_words, tab2_scales, tab3_words, tab3_scales,
+    offs, offs2, offs3, w1, w2_words, w2_scales, w3, gain, avail, out,
+):
+    nc = tc.nc
+    with ExitStack() as ctx:
+        keep = ctx.enter_context(tc.tile_pool(name="keep", bufs=1))
+        ring = ctx.enter_context(tc.tile_pool(name="ring", bufs=3))
+        psum = ctx.enter_context(tc.psum_pool(name="psum", bufs=2))
+
+        def load_list(name, src):
+            t = keep.tile([P, S // 16], U16, name=name)
+            nc.sync.dma_start(t[:], src)
+            return t
+
+        def load_words(name, src, a):
+            t = keep.tile([P, T], I32, name=name, align_bytes=64)
+            nc.sync.dma_start(t[:], src[a].rearrange("p t i -> p (t i)").bitcast(I32))
+            return t
+
+        def zeroed_scale_tile(name, cols):
+            t = keep.tile([P, cols], U8, name=name, align_bytes=64)
+            nc.gpsimd.memset(t[:].bitcast(I32), 0)
+            return t
+
+        def load_side_by_side_quadrant(queue, t, src, q):
+            queue.dma_start(
+                t[32 * q : 32 * q + 4, :].bitcast(I32).rearrange("p (a w) -> p a w", a=PASSES),
+                src.bitcast(I32)[:, 4 * q : 4 * q + 4, :].rearrange("a r w -> r a w"),
+            )
+
+        def load_stacked_quadrant(t, src, q):
+            nc.sync.dma_start(
+                t[32 * q : 32 * q + 8, :].bitcast(I32),
+                src.bitcast(I32)[:, 4 * q : 4 * q + 4, :],
+            )
+
+        def load_weight(name, w, a, b):
+            t = ring.tile([P, PACK, KP], F32, name=name, tag="w_raw", bufs=6, align_bytes=64)
+            nc.sync.dma_start(
+                t[:], w[KP * a : KP * (a + 1), KP * b : KP * (b + 1)].rearrange("(p i) c -> p i c", i=PACK)
+            )
+            return t
+
+        def gather_words(name, words, lst, pieces=1):
+            g = keep.tile([P, S], U32, name=name, align_bytes=64)
+            n = S // pieces
+            for u in range(pieces):
+                nc.vector.tensor_copy(
+                    g[:, n * u : n * (u + 1)],
+                    words[:].bitcast(U32).indirect(lst[:, n // 16 * u : n // 16 * (u + 1)]),
+                )
+            return g
+
+        def gather_bytes(name, window, lst):
+            g = keep.tile([P, S], U8, name=name, align_bytes=64)
+            nc.vector.tensor_copy(g[:], window.indirect(lst[:]))
+            return g
+
+        def round_weight(raw, scalar_cols):
+            g = ring.tile([P, KP, PACK], BF16, name="w_bf16", align_bytes=64)
+            src = raw[:].rearrange("p i (c e) -> p c i e", e=4)
+            dst = g[:].rearrange("p (c e) i -> p c i e", e=4)
+            cut = scalar_cols // 4
+            nc.scalar.activation(dst[:, :cut], src[:, :cut], ACT.Copy)
+            if scalar_cols < KP:
+                nc.vector.tensor_copy(dst[:, cut:], src[:, cut:])
+            return g
+
+        def quantise(name, grouped):
+            codes = keep.tile([P, KP], U32, name=name + "_codes", align_bytes=64)
+            scales = keep.tile([P, KP], U8, name=name + "_scales", align_bytes=64)
+            nc.vector.quantize_mx(
+                out=codes[:].bitcast(FP8X4), scales=scales[:], in_=grouped[:].rearrange("p c i -> p (c i)")
+            )
+            return codes, scales
+
+        v_scale_rows = zeroed_scale_tile("v_scale_rows", PASSES * T)
+        w2_scale = zeroed_scale_tile("w2_scale", PASSES * H)
+        v2_scale_rows = zeroed_scale_tile("v2_scale_rows", T)
+        v3_scale_rows = zeroed_scale_tile("v3_scale_rows", T)
+        identity = keep.tile([P, P], F32, name="identity")
+        make_identity(nc, identity[:])
+
+        idx = load_list("idx", offs)
+        idx2 = load_list("idx2", offs2)
+        idx3 = load_list("idx3", offs3)
+        gain_sb = keep.tile([P, PASSES, PACK], F32, name="gain_sb")
+        nc.sync.dma_start(gain_sb[:], gain.rearrange("(b p i) -> p b i", b=PASSES, i=PACK))
+        raw = {}
+        raw[1, 0, 0] = load_weight("w1_00", w1, 0, 0)
+        v_words = [load_words("v_words0", tab_words, 0)]
+        w2_codes = []
+        for a in range(PASSES):
+            t = keep.tile([P, 2 * H], U8, name="w2_codes%d" % a, align_bytes=64)
+            nc.sync.dma_start(t[:].bitcast(I32), w2_words[a].bitcast(I32))
+            w2_codes.append(t)
+        for q in range(4):
+            load_side_by_side_quadrant(nc.scalar, v_scale_rows, tab_scales, q)
+        v_words.append(load_words("v_words1", tab_words, 1))
+        for q in range(4):
+            load_side_by_side_quadrant(nc.sync, w2_scale, w2_scales, q)
+        raw[1, 1, 0] = load_weight("w1_10", w1, 1, 0)
+        for q in range(2):
+            load_stacked_quadrant(v2_scale_rows, tab2_scales, q)
+        raw[3, 0, 0] = load_weight("w3_00", w3, 0, 0)
+        for q in range(2, 4):
+            load_stacked_quadrant(v2_scale_rows, tab2_scales, q)
+        for q in range(2):
+            load_stacked_quadrant(v3_scale_rows, tab3_scales, q)
+        raw[3, 1, 0] = load_weight("w3_10", w3, 1, 0)
+        for q in range(2, 4):
+            load_stacked_quadrant(v3_scale_rows, tab3_scales, q)
+        for which, w in ((1, w1), (3, w3)):
+            for a in range(PASSES):
+                raw[which, a, 1] = load_weight("w%d_%d1" % (which, a), w, a, 1)
+        v2_words = [load_words("v2_words%d" % b, tab2_words, b) for b in range(PASSES)]
+        v3_words = [load_words("v3_words%d" % b, tab3_words, b) for b in range(PASSES)]
+        avail_sb = []
+        for mt in range(TILES):
+            t = keep.tile([P, S], F32, name="avail%d" % mt)
+            nc.sync.dma_start(t[:], avail[P * mt : P * (mt + 1), :])
+            avail_sb.append(t)
+
+        def by_byte(bank):
+            return bank[:].rearrange("j (p i) -> j i p", i=PACK)
+
+        wq = {}
+        v = []
+
+        def product(bank, jt, moving):
+            cols = slice(P * jt, P * (jt + 1))
+            for a in range(PASSES):
+                codes, scales = moving(a)
+                nc.tensor.matmul_mx(
+                    out=bank[:], lhsT=v[a][:, cols].bitcast(FP8X4), lhsT_scale=v_scale[a][:, cols],
+                    rhs=codes, rhs_scale=scales, start=(a == 0), stop=(a == PASSES - 1),
+                )
+
+        def quantised_weight(which, b):
+            return lambda a: (wq[which, a, b][0][:].bitcast(FP8X4), wq[which, a, b][1][:])
+
+        def packed_weight(b):
+            return lambda a: (
+                w2_codes[a][:, 2 * KP * b : 2 * KP * (b + 1)].bitcast(FP4X4),
+                w2_scale[:, H * a + KP * b : H * a + KP * (b + 1)],
+            )
+
+        def d2_to_sbuf(b, jt):
+            d2 = psum.tile([P, KP], F32, name="bank_b")
+            product(d2, jt, packed_weight(b))
+            d2_sb = keep.tile([P, PACK, P], F32, name="larger%d%d" % (b, jt), tag="larger%d%d" % (b, jt))
+            nc.scalar.activation(d2_sb[:], by_byte(d2), ACT.Copy)
+            return d2_sb
+
+        def larger_with_d1(b, jt, larger):
+            d1 = psum.tile([P, KP], F32, name="bank_a")
+            product(d1, jt, quantised_weight(1, b))
+            nc.vector.tensor_tensor(larger[:], by_byte(d1), larger[:], ALU.max)
+
+        def tanh_of_d3(b, jt):
+            d3 = psum.tile([P, KP], F32, name="bank_c")
+            product(d3, jt, quantised_weight(3, b))
+            th = ring.tile([P, PACK, P], F32, name="tanh_sb")
+            nc.scalar.activation(th[:], by_byte(d3), ACT.Tanh)
+            return th
+
+        def turn_and_round(b, jt, larger, th, h_bf16):
+            total = psum.tile([P, KP], F32, name="bank_d")
+            for i in range(PACK):
+                cols = slice(P * i, P * (i + 1))
+                nc.tensor.matmul(total[:, cols], larger[:, i, :], identity[:], start=True, stop=False, is_transpose=True)
+                nc.tensor.matmul(total[:, cols], th[:, i, :], identity[:], start=False, stop=True, is_transpose=True)
+            nc.vector.tensor_tensor(
+                h_bf16[:, P * jt : P * (jt + 1), :],
+                total[:].rearrange("p (i j) -> p j i", i=PACK),
+                gain_sb[:, b : b + 1, :].to_broadcast([P, P, PACK]),
+                ALU.mult,
+            )
+
+        def prepare_weight(which, a, b, scalar_cols=SCALAR_COLS):
+            g = round_weight(raw[which, a, b], scalar_cols)
+            wq[which, a, b] = quantise("w%d_%d%d" % (which, a, b), g)
+
+        def second_half(b, larger):
+            h_bf16 = keep.tile([P, S, PACK], BF16, name="h_bf16_%d" % b, align_bytes=64)
+            th = [tanh_of_d3(b, 0)]
+            for jt in range(TILES):
+                if jt + 1 < TILES:
+                    th.append(tanh_of_d3(b, jt + 1))
+                turn_and_round(b, jt, larger[jt], th[jt], h_bf16)
+            return quantise("h%d" % b, h_bf16)
+
+        prepare_weight(1, 0, 0, KP)
+        v.append(gather_words("v0", v_words[0], idx))
+        v_scale = [gather_bytes("v_scale%d" % a, v_scale_rows[:, T * a : T * (a + 1)], idx) for a in range(PASSES)]
+        v.append(gather_words("v1", v_words[1], idx))
+        prepare_weight(1, 1, 0)
+        larger0 = [d2_to_sbuf(0, jt) for jt in range(TILES)]
+        prepare_weight(3, 0, 0)
+        for jt in range(TILES):
+            larger_with_d1(0, jt, larger0[jt])
+        prepare_weight(3, 1, 0)
+        v2_scale = gather_bytes("v2_scale", v2_scale_rows[:], idx2)
+        prepare_weight(1, 0, 1)
+        hq = [second_half(0, larger0)]
+        prepare_weight(1, 1, 1)
+        v3_scale = gather_bytes("v3_scale", v3_scale_rows[:], idx3)
+        larger1 = [d2_to_sbuf(1, jt) for jt in range(TILES)]
+        prepare_weight(3, 0, 1)
+        for jt in range(TILES):
+            larger_with_d1(1, jt, larger1[jt])
+        prepare_weight(3, 1, 1, SCALAR_COLS_LAST)
+        hq.append(second_half(1, larger1))
+        v2 = [gather_words("v2_%d" % b, v2_words[b], idx2) for b in range(PASSES)]
+        v3 = [gather_words("v3_0", v3_words[0], idx3)]
+
+        def score_pass(bank, cand, cand_scale, mt, b):
+            cols = slice(P * mt, P * (mt + 1))
+            nc.tensor.matmul_mx(
+                out=bank[:], lhsT=cand[b][:, cols].bitcast(FP8X4), lhsT_scale=cand_scale[4 * b : P, cols],
+                rhs=hq[b][0][:].bitcast(FP8X4), rhs_scale=hq[b][1][:], start=(b == 0), stop=(b == PASSES - 1),
+            )
+
+        e2 = [psum.tile([P, KP], F32, name=("bank_a", "bank_b")[mt % 2]) for mt in range(TILES)]
+        for b in range(PASSES):
+            for mt in range(TILES):
+                score_pass(e2[mt], v2, v2_scale, mt, b)
+        e2_sb = []
+        for mt in range(TILES):
+            t = keep.tile([P, S], F32, name="e2_sb%d" % mt, tag="larger0%d" % mt)
+            nc.scalar.activation(t[:], e2[mt][:], ACT.Copy)
+            e2_sb.append(t)
+        e3 = [psum.tile([P, KP], F32, name=("bank_c", "bank_d")[mt % 2]) for mt in range(TILES)]
+        for mt in range(TILES):
+            score_pass(e3[mt], v3, v3_scale, mt, 0)
+        v3.append(gather_words("v3_1", v3_words[1], idx3, pieces=TILES))
+        for mt in range(TILES):
+            score_pass(e3[mt], v3, v3_scale, mt, 1)
+            best = ring.tile([P, S], F32, name="best")
+            nc.vector.tensor_tensor(best[:], e3[mt][:], e2_sb[mt][:], ALU.max)
+            result = keep.tile([P, S], F32, name="result%d" % mt)
+            nc.vector.tensor_tensor(result[:], best[:], avail_sb[mt][:], ALU.mult)
+            nc.sync.dma_start(out[P * mt : P * (mt + 1), :], result[:])

@@ -34,21 +34,21 @@ def tile_list_staffing_team_scores_kernel(
     with ExitStack() as ctx:
         keep = ctx.enter_context(tc.tile_pool(name="keep", bufs=1))
         ring = ctx.enter_context(tc.tile_pool(name="ring", bufs=3))
-        psum = ctx.enter_context(tc.psum_pool(name="psum", bufs=2))
+        psum = ctx.enter_context(tc.psum_pool(name="psum", bufs=1))
 
         def load_list(name, src):
             t = keep.tile([P, S // 16], U16, name=name)
             nc.sync.dma_start(t[:], src)
             return t
 
-        def load_words(name, src, a):
+        def load_words(name, src, a, queue):
             t = keep.tile([P, T], I32, name=name, align_bytes=64)
-            nc.sync.dma_start(t[:], src[a].rearrange("p t i -> p (t i)").bitcast(I32))
+            queue.dma_start(t[:], src[a].rearrange("p t i -> p (t i)").bitcast(I32))
             return t
 
-        def zeroed_scale_tile(name, cols):
+        def zeroed_scale_tile(name, cols, engine):
             t = keep.tile([P, cols], U8, name=name, align_bytes=64)
-            nc.gpsimd.memset(t[:].bitcast(I32), 0)
+            engine.memset(t[:].bitcast(I32), 0)
             return t
 
         def load_side_by_side_quadrant(queue, t, src, q):
@@ -57,8 +57,8 @@ def tile_list_staffing_team_scores_kernel(
                 src.bitcast(I32)[:, 4 * q : 4 * q + 4, :].rearrange("a r w -> r a w"),
             )
 
-        def load_stacked_quadrant(t, src, q):
-            nc.sync.dma_start(
+        def load_stacked_quadrant(queue, t, src, q):
+            queue.dma_start(
                 t[32 * q : 32 * q + 8, :].bitcast(I32),
                 src.bitcast(I32)[:, 4 * q : 4 * q + 4, :],
             )
@@ -92,7 +92,9 @@ def tile_list_staffing_team_scores_kernel(
             cut = scalar_cols // 4
             nc.scalar.activation(dst[:, :cut], src[:, :cut], ACT.Copy)
             if scalar_cols < KP:
-                nc.vector.tensor_copy(dst[:, cut:], src[:, cut:])
+                nc.gpsimd.tensor_scalar(
+                    g[:, scalar_cols:, :], raw[:, :, scalar_cols:].rearrange("p i c -> p c i"), 1.0, 0.0, ALU.mult, ALU.add
+                )
             return g
 
         def quantise(name, grouped):
@@ -103,52 +105,59 @@ def tile_list_staffing_team_scores_kernel(
             )
             return codes, scales
 
-        v_scale_rows = zeroed_scale_tile("v_scale_rows", PASSES * T)
-        w2_scale = zeroed_scale_tile("w2_scale", PASSES * H)
-        v2_scale_rows = zeroed_scale_tile("v2_scale_rows", T)
-        v3_scale_rows = zeroed_scale_tile("v3_scale_rows", T)
+        v_scale_rows = zeroed_scale_tile("v_scale_rows", PASSES * T, nc.gpsimd)
+        w2_scale = zeroed_scale_tile("w2_scale", PASSES * H, nc.gpsimd)
+        v2_scale_rows = zeroed_scale_tile("v2_scale_rows", T, nc.vector)
+        v3_scale_rows = zeroed_scale_tile("v3_scale_rows", T, nc.vector)
+
+        def load_w2_codes(b, queue):
+            t = keep.tile([P, PASSES, 2 * KP], U8, name="w2_codes%d" % b, align_bytes=64)
+            queue.dma_start(
+                t[:].bitcast(I32), w2_words[:, :, 2 * KP * b : 2 * KP * (b + 1)].bitcast(I32).rearrange("a p w -> p a w")
+            )
+            return t
+
+        for q in range(4):
+            load_side_by_side_quadrant((nc.scalar, nc.gpsimd)[q // 2], v_scale_rows, tab_scales, q)
+        w2_codes = []
+        for q in range(4):
+            load_side_by_side_quadrant(nc.scalar, w2_scale, w2_scales, q)
+        for q in range(4):
+            load_stacked_quadrant(nc.gpsimd, v2_scale_rows, tab2_scales, q)
+        for q in range(4):
+            load_stacked_quadrant(nc.gpsimd, v3_scale_rows, tab3_scales, q)
         identity = keep.tile([P, P], F32, name="identity")
         make_identity(nc, identity[:])
+        gain_sb = keep.tile([P, PASSES, PACK], F32, name="gain_sb")
+        nc.gpsimd.dma_start(gain_sb[:], gain.rearrange("(b p i) -> p b i", b=PASSES, i=PACK))
+        v_words = []
 
         idx = load_list("idx", offs)
+        raw = {}
+        v_words.append(load_words("v_words0", tab_words, 0, nc.sync))
+        raw[1, 0, 0] = load_weight("w1_00", w1, 0, 0)
+        v_words.append(load_words("v_words1", tab_words, 1, nc.sync))
         idx2 = load_list("idx2", offs2)
         idx3 = load_list("idx3", offs3)
-        gain_sb = keep.tile([P, PASSES, PACK], F32, name="gain_sb")
-        nc.sync.dma_start(gain_sb[:], gain.rearrange("(b p i) -> p b i", b=PASSES, i=PACK))
-        raw = {}
-        raw[1, 0, 0] = load_weight("w1_00", w1, 0, 0)
-        v_words = [load_words("v_words0", tab_words, 0)]
-        w2_codes = []
-        for a in range(PASSES):
-            t = keep.tile([P, 2 * H], U8, name="w2_codes%d" % a, align_bytes=64)
-            nc.sync.dma_start(t[:].bitcast(I32), w2_words[a].bitcast(I32))
-            w2_codes.append(t)
-        for q in range(4):
-            load_side_by_side_quadrant(nc.scalar, v_scale_rows, tab_scales, q)
-        v_words.append(load_words("v_words1", tab_words, 1))
-        for q in range(4):
-            load_side_by_side_quadrant(nc.sync, w2_scale, w2_scales, q)
         raw[1, 1, 0] = load_weight("w1_10", w1, 1, 0)
-        for q in range(2):
-            load_stacked_quadrant(v2_scale_rows, tab2_scales, q)
+        w2_codes.append(load_w2_codes(0, nc.sync))
+        w2_codes.append(load_w2_codes(1, nc.sync))
+        raw[1, 0, 1] = load_weight("w1_01", w1, 0, 1)
+        raw[1, 1, 1] = load_weight("w1_11", w1, 1, 1)
         raw[3, 0, 0] = load_weight("w3_00", w3, 0, 0)
-        for q in range(2, 4):
-            load_stacked_quadrant(v2_scale_rows, tab2_scales, q)
-        for q in range(2):
-            load_stacked_quadrant(v3_scale_rows, tab3_scales, q)
         raw[3, 1, 0] = load_weight("w3_10", w3, 1, 0)
-        for q in range(2, 4):
-            load_stacked_quadrant(v3_scale_rows, tab3_scales, q)
-        for which, w in ((1, w1), (3, w3)):
-            for a in range(PASSES):
-                raw[which, a, 1] = load_weight("w%d_%d1" % (which, a), w, a, 1)
-        v2_words = [load_words("v2_words%d" % b, tab2_words, b) for b in range(PASSES)]
-        v3_words = [load_words("v3_words%d" % b, tab3_words, b) for b in range(PASSES)]
+        raw[3, 0, 1] = load_weight("w3_01", w3, 0, 1)
+        raw[3, 1, 1] = load_weight("w3_11", w3, 1, 1)
+        v2_words = [load_words("v2_words%d" % b, tab2_words, b, nc.sync) for b in range(PASSES)]
+        v3_words = [load_words("v3_words%d" % b, tab3_words, b, nc.sync) for b in range(PASSES)]
         avail_sb = []
         for mt in range(TILES):
             t = keep.tile([P, S], F32, name="avail%d" % mt)
             nc.sync.dma_start(t[:], avail[P * mt : P * (mt + 1), :])
             avail_sb.append(t)
+
+        def bank(n):
+            return psum.tile([P, KP], F32, name="bank%d" % n)
 
         def by_byte(bank):
             return bank[:].rearrange("j (p i) -> j i p", i=PACK)
@@ -170,35 +179,37 @@ def tile_list_staffing_team_scores_kernel(
 
         def packed_weight(b):
             return lambda a: (
-                w2_codes[a][:, 2 * KP * b : 2 * KP * (b + 1)].bitcast(FP4X4),
+                w2_codes[b][:, a, :].bitcast(FP4X4),
                 w2_scale[:, H * a + KP * b : H * a + KP * (b + 1)],
             )
 
         def d2_to_sbuf(b, jt):
-            d2 = psum.tile([P, KP], F32, name="bank_b")
+            d2 = bank(jt)
             product(d2, jt, packed_weight(b))
             d2_sb = keep.tile([P, PACK, P], F32, name="larger%d%d" % (b, jt), tag="larger%d%d" % (b, jt))
             nc.scalar.activation(d2_sb[:], by_byte(d2), ACT.Copy)
             return d2_sb
 
         def larger_with_d1(b, jt, larger):
-            d1 = psum.tile([P, KP], F32, name="bank_a")
+            d1 = bank(4 + jt)
             product(d1, jt, quantised_weight(1, b))
             nc.vector.tensor_tensor(larger[:], by_byte(d1), larger[:], ALU.max)
 
-        def tanh_of_d3(b, jt):
-            d3 = psum.tile([P, KP], F32, name="bank_c")
+        def tanh_of_d3(b, jt, n):
+            d3 = bank(n)
             product(d3, jt, quantised_weight(3, b))
-            th = ring.tile([P, PACK, P], F32, name="tanh_sb")
+            th = ring.tile([P, PACK, P], F32, name="tanh_sb", bufs=4)
             nc.scalar.activation(th[:], by_byte(d3), ACT.Tanh)
             return th
 
-        def turn_and_round(b, jt, larger, th, h_bf16):
-            total = psum.tile([P, KP], F32, name="bank_d")
-            for i in range(PACK):
-                cols = slice(P * i, P * (i + 1))
-                nc.tensor.matmul(total[:, cols], larger[:, i, :], identity[:], start=True, stop=False, is_transpose=True)
-                nc.tensor.matmul(total[:, cols], th[:, i, :], identity[:], start=False, stop=True, is_transpose=True)
+        def turn_and_round(b, jt, n, first, second, h_bf16):
+            total = bank(n)
+            for term, opens in ((first, True), (second, False)):
+                for i in range(PACK):
+                    nc.tensor.matmul(
+                        total[:, P * i : P * (i + 1)], term[:, i, :], identity[:],
+                        start=(opens and i == 0), stop=(not opens and i == PACK - 1), is_transpose=True,
+                    )
             nc.vector.tensor_tensor(
                 h_bf16[:, P * jt : P * (jt + 1), :],
                 total[:].rearrange("p (i j) -> p j i", i=PACK),
@@ -206,67 +217,65 @@ def tile_list_staffing_team_scores_kernel(
                 ALU.mult,
             )
 
-        def prepare_weight(which, a, b, scalar_cols=SCALAR_COLS):
+        def prepare_weight(which, a, b, scalar_cols):
             g = round_weight(raw[which, a, b], scalar_cols)
             wq[which, a, b] = quantise("w%d_%d%d" % (which, a, b), g)
 
-        def second_half(b, larger):
+        def second_half(b, larger, d3_banks, total_banks):
             h_bf16 = keep.tile([P, S, PACK], BF16, name="h_bf16_%d" % b, align_bytes=64)
-            th = [tanh_of_d3(b, 0)]
+            th = [tanh_of_d3(b, 0, d3_banks[0])]
             for jt in range(TILES):
                 if jt + 1 < TILES:
-                    th.append(tanh_of_d3(b, jt + 1))
-                turn_and_round(b, jt, larger[jt], th[jt], h_bf16)
+                    th.append(tanh_of_d3(b, jt + 1, d3_banks[jt + 1]))
+                turn_and_round(b, jt, total_banks[jt], larger[jt], th[jt], h_bf16)
             return quantise("h%d" % b, h_bf16)
 
-        prepare_weight(1, 0, 0, KP)
         v.append(gather_words("v0", v_words[0], idx))
         v_scale = [gather_bytes("v_scale%d" % a, v_scale_rows[:, T * a : T * (a + 1)], idx) for a in range(PASSES)]
         v.append(gather_words("v1", v_words[1], idx))
-        prepare_weight(1, 1, 0)
+        prepare_weight(1, 0, 0, 512)
+        prepare_weight(1, 1, 0, 256)
+        v2_scale = gather_bytes("v2_scale", v2_scale_rows[:], idx2)
+        v3_scale = gather_bytes("v3_scale", v3_scale_rows[:], idx3)
+        prepare_weight(1, 0, 1, 256)
         larger0 = [d2_to_sbuf(0, jt) for jt in range(TILES)]
-        prepare_weight(3, 0, 0)
+        prepare_weight(1, 1, 1, 256)
         for jt in range(TILES):
             larger_with_d1(0, jt, larger0[jt])
-        prepare_weight(3, 1, 0)
-        v2_scale = gather_bytes("v2_scale", v2_scale_rows[:], idx2)
-        prepare_weight(1, 0, 1)
-        hq = [second_half(0, larger0)]
-        prepare_weight(1, 1, 1)
-        v3_scale = gather_bytes("v3_scale", v3_scale_rows[:], idx3)
+        prepare_weight(3, 0, 0, 256)
         larger1 = [d2_to_sbuf(1, jt) for jt in range(TILES)]
-        prepare_weight(3, 0, 1)
+        prepare_weight(3, 1, 0, 256)
         for jt in range(TILES):
             larger_with_d1(1, jt, larger1[jt])
-        prepare_weight(3, 1, 1, SCALAR_COLS_LAST)
-        hq.append(second_half(1, larger1))
+        prepare_weight(3, 0, 1, 256)
+        prepare_weight(3, 1, 1, 256)
+        hq = [second_half(0, larger0, (0, 1, 2, 3), (4, 5, 6, 7))]
+        hq.append(second_half(1, larger1, (0, 1, 2, 3), (4, 5, 6, 7)))
         v2 = [gather_words("v2_%d" % b, v2_words[b], idx2) for b in range(PASSES)]
         v3 = [gather_words("v3_0", v3_words[0], idx3)]
 
-        def score_pass(bank, cand, cand_scale, mt, b):
+        def score_pass(acc, cand, cand_scale, mt, b):
             cols = slice(P * mt, P * (mt + 1))
             nc.tensor.matmul_mx(
-                out=bank[:], lhsT=cand[b][:, cols].bitcast(FP8X4), lhsT_scale=cand_scale[4 * b : P, cols],
+                out=acc[:], lhsT=cand[b][:, cols].bitcast(FP8X4), lhsT_scale=cand_scale[4 * b : P, cols],
                 rhs=hq[b][0][:].bitcast(FP8X4), rhs_scale=hq[b][1][:], start=(b == 0), stop=(b == PASSES - 1),
             )
 
-        e2 = [psum.tile([P, KP], F32, name=("bank_a", "bank_b")[mt % 2]) for mt in range(TILES)]
-        for b in range(PASSES):
-            for mt in range(TILES):
-                score_pass(e2[mt], v2, v2_scale, mt, b)
         e2_sb = []
         for mt in range(TILES):
+            e2 = bank(mt)
+            for b in range(PASSES):
+                score_pass(e2, v2, v2_scale, mt, b)
             t = keep.tile([P, S], F32, name="e2_sb%d" % mt, tag="larger0%d" % mt)
-            nc.scalar.activation(t[:], e2[mt][:], ACT.Copy)
+            nc.scalar.activation(t[:], e2[:], ACT.Copy)
             e2_sb.append(t)
-        e3 = [psum.tile([P, KP], F32, name=("bank_c", "bank_d")[mt % 2]) for mt in range(TILES)]
+        v3.append(gather_words("v3_1", v3_words[1], idx3, pieces=4))
         for mt in range(TILES):
-            score_pass(e3[mt], v3, v3_scale, mt, 0)
-        v3.append(gather_words("v3_1", v3_words[1], idx3, pieces=TILES))
-        for mt in range(TILES):
-            score_pass(e3[mt], v3, v3_scale, mt, 1)
-            best = ring.tile([P, S], F32, name="best")
-            nc.vector.tensor_tensor(best[:], e3[mt][:], e2_sb[mt][:], ALU.max)
+            e3 = bank(4 + mt)
+            for b in range(PASSES):
+                score_pass(e3, v3, v3_scale, mt, b)
+            best = ring.tile([P, S], F32, name="best", bufs=4)
+            nc.vector.tensor_tensor(best[:], e3[:], e2_sb[mt][:], ALU.max)
             result = keep.tile([P, S], F32, name="result%d" % mt)
-            nc.vector.tensor_tensor(result[:], best[:], avail_sb[mt][:], ALU.mult)
+            (nc.gpsimd if mt < 2 else nc.vector).tensor_tensor(result[:], best[:], avail_sb[mt][:], ALU.mult)
             nc.sync.dma_start(out[P * mt : P * (mt + 1), :], result[:])

@@ -85,16 +85,24 @@ def tile_list_staffing_team_scores_kernel(
             nc.vector.tensor_copy(g[:], window.indirect(lst[:]))
             return g
 
-        def round_weight(raw, scalar_cols):
+        def by_neighbours(grouped, raw, cols):
+            return (
+                grouped[:, cols, :].rearrange("p (c e) i -> p c i e", e=4),
+                raw[:, :, cols].rearrange("p i (c e) -> p c i e", e=4),
+            )
+
+        def round_on_vector(grouped, raw, cols):
+            nc.vector.tensor_copy(*by_neighbours(grouped, raw, cols))
+
+        def round_on_gpsimd(grouped, raw, cols):
+            nc.gpsimd.tensor_scalar(
+                grouped[:, cols, :], raw[:, :, cols].rearrange("p i c -> p c i"), 1.0, 0.0, ALU.mult, ALU.add
+            )
+
+        def round_weight(raw, scalar_cols, round_rest):
             g = ring.tile([P, KP, PACK], BF16, name="w_bf16", align_bytes=64)
-            src = raw[:].rearrange("p i (c e) -> p c i e", e=4)
-            dst = g[:].rearrange("p (c e) i -> p c i e", e=4)
-            cut = scalar_cols // 4
-            nc.scalar.activation(dst[:, :cut], src[:, :cut], ACT.Copy)
-            if scalar_cols < KP:
-                nc.gpsimd.tensor_scalar(
-                    g[:, scalar_cols:, :], raw[:, :, scalar_cols:].rearrange("p i c -> p c i"), 1.0, 0.0, ALU.mult, ALU.add
-                )
+            nc.scalar.activation(*by_neighbours(g, raw, slice(0, scalar_cols)), ACT.Copy)
+            round_rest(g, raw, slice(scalar_cols, KP))
             return g
 
         def quantise(name, grouped):
@@ -110,16 +118,8 @@ def tile_list_staffing_team_scores_kernel(
         v2_scale_rows = zeroed_scale_tile("v2_scale_rows", T, nc.vector)
         v3_scale_rows = zeroed_scale_tile("v3_scale_rows", T, nc.vector)
 
-        def load_w2_codes(b, queue):
-            t = keep.tile([P, PASSES, 2 * KP], U8, name="w2_codes%d" % b, align_bytes=64)
-            queue.dma_start(
-                t[:].bitcast(I32), w2_words[:, :, 2 * KP * b : 2 * KP * (b + 1)].bitcast(I32).rearrange("a p w -> p a w")
-            )
-            return t
-
         for q in range(4):
-            load_side_by_side_quadrant((nc.scalar, nc.gpsimd)[q // 2], v_scale_rows, tab_scales, q)
-        w2_codes = []
+            load_side_by_side_quadrant(nc.scalar, v_scale_rows, tab_scales, q)
         for q in range(4):
             load_side_by_side_quadrant(nc.scalar, w2_scale, w2_scales, q)
         for q in range(4):
@@ -135,14 +135,14 @@ def tile_list_staffing_team_scores_kernel(
         idx = load_list("idx", offs)
         raw = {}
         v_words.append(load_words("v_words0", tab_words, 0, nc.sync))
-        raw[1, 0, 0] = load_weight("w1_00", w1, 0, 0)
+        w2_codes = keep.tile([P, PASSES, 2 * H], U8, name="w2_codes", align_bytes=64)
+        nc.sync.dma_start(w2_codes[:].bitcast(I32), w2_words.bitcast(I32).rearrange("a p w -> p a w"))
         v_words.append(load_words("v_words1", tab_words, 1, nc.sync))
         idx2 = load_list("idx2", offs2)
-        idx3 = load_list("idx3", offs3)
+        raw[1, 0, 0] = load_weight("w1_00", w1, 0, 0)
         raw[1, 1, 0] = load_weight("w1_10", w1, 1, 0)
-        w2_codes.append(load_w2_codes(0, nc.sync))
-        w2_codes.append(load_w2_codes(1, nc.sync))
         raw[1, 0, 1] = load_weight("w1_01", w1, 0, 1)
+        idx3 = load_list("idx3", offs3)
         raw[1, 1, 1] = load_weight("w1_11", w1, 1, 1)
         raw[3, 0, 0] = load_weight("w3_00", w3, 0, 0)
         raw[3, 1, 0] = load_weight("w3_10", w3, 1, 0)
@@ -179,7 +179,7 @@ def tile_list_staffing_team_scores_kernel(
 
         def packed_weight(b):
             return lambda a: (
-                w2_codes[b][:, a, :].bitcast(FP4X4),
+                w2_codes[:, a, 2 * KP * b : 2 * KP * (b + 1)].bitcast(FP4X4),
                 w2_scale[:, H * a + KP * b : H * a + KP * (b + 1)],
             )
 
@@ -217,8 +217,8 @@ def tile_list_staffing_team_scores_kernel(
                 ALU.mult,
             )
 
-        def prepare_weight(which, a, b, scalar_cols):
-            g = round_weight(raw[which, a, b], scalar_cols)
+        def prepare_weight(which, a, b, scalar_cols, round_rest):
+            g = round_weight(raw[which, a, b], scalar_cols, round_rest)
             wq[which, a, b] = quantise("w%d_%d%d" % (which, a, b), g)
 
         def second_half(b, larger, d3_banks, total_banks):
@@ -233,49 +233,49 @@ def tile_list_staffing_team_scores_kernel(
         v.append(gather_words("v0", v_words[0], idx))
         v_scale = [gather_bytes("v_scale%d" % a, v_scale_rows[:, T * a : T * (a + 1)], idx) for a in range(PASSES)]
         v.append(gather_words("v1", v_words[1], idx))
-        prepare_weight(1, 0, 0, 512)
-        prepare_weight(1, 1, 0, 256)
-        v2_scale = gather_bytes("v2_scale", v2_scale_rows[:], idx2)
-        v3_scale = gather_bytes("v3_scale", v3_scale_rows[:], idx3)
-        prepare_weight(1, 0, 1, 256)
+        prepare_weight(1, 0, 0, 256, round_on_vector)
+        prepare_weight(1, 1, 0, 256, round_on_vector)
+        prepare_weight(1, 0, 1, 256, round_on_vector)
+        prepare_weight(1, 1, 1, 256, round_on_vector)
+        prepare_weight(3, 0, 0, 256, round_on_vector)
+        prepare_weight(3, 1, 0, 256, round_on_vector)
+        prepare_weight(3, 0, 1, 256, round_on_vector)
+        prepare_weight(3, 1, 1, 192, round_on_vector)
         larger0 = [d2_to_sbuf(0, jt) for jt in range(TILES)]
-        prepare_weight(1, 1, 1, 256)
+        larger1 = [d2_to_sbuf(1, jt) for jt in range(TILES)]
         for jt in range(TILES):
             larger_with_d1(0, jt, larger0[jt])
-        prepare_weight(3, 0, 0, 256)
-        larger1 = [d2_to_sbuf(1, jt) for jt in range(TILES)]
-        prepare_weight(3, 1, 0, 256)
         for jt in range(TILES):
             larger_with_d1(1, jt, larger1[jt])
-        prepare_weight(3, 0, 1, 256)
-        prepare_weight(3, 1, 1, 256)
         hq = [second_half(0, larger0, (0, 1, 2, 3), (4, 5, 6, 7))]
         hq.append(second_half(1, larger1, (0, 1, 2, 3), (4, 5, 6, 7)))
+        v2_scale = gather_bytes("v2_scale", v2_scale_rows[:], idx2)
+        v3_scale = gather_bytes("v3_scale", v3_scale_rows[:], idx3)
         v2 = [gather_words("v2_%d" % b, v2_words[b], idx2) for b in range(PASSES)]
         v3 = [gather_words("v3_0", v3_words[0], idx3)]
 
-        def score_pass(acc, cand, cand_scale, mt, b):
+        def score_pass(acc, cand, cand_scale, mt, b, opens):
             cols = slice(P * mt, P * (mt + 1))
             nc.tensor.matmul_mx(
                 out=acc[:], lhsT=cand[b][:, cols].bitcast(FP8X4), lhsT_scale=cand_scale[4 * b : P, cols],
-                rhs=hq[b][0][:].bitcast(FP8X4), rhs_scale=hq[b][1][:], start=(b == 0), stop=(b == PASSES - 1),
+                rhs=hq[b][0][:].bitcast(FP8X4), rhs_scale=hq[b][1][:], start=opens, stop=not opens,
             )
 
         e2_sb = []
         for mt in range(TILES):
             e2 = bank(mt)
             for b in range(PASSES):
-                score_pass(e2, v2, v2_scale, mt, b)
+                score_pass(e2, v2, v2_scale, mt, b, b == 0)
             t = keep.tile([P, S], F32, name="e2_sb%d" % mt, tag="larger0%d" % mt)
             nc.scalar.activation(t[:], e2[:], ACT.Copy)
             e2_sb.append(t)
         v3.append(gather_words("v3_1", v3_words[1], idx3, pieces=4))
         for mt in range(TILES):
             e3 = bank(4 + mt)
-            for b in range(PASSES):
-                score_pass(e3, v3, v3_scale, mt, b)
+            for b in (1, 0):
+                score_pass(e3, v3, v3_scale, mt, b, b == 1)
             best = ring.tile([P, S], F32, name="best", bufs=4)
             nc.vector.tensor_tensor(best[:], e3[:], e2_sb[mt][:], ALU.max)
             result = keep.tile([P, S], F32, name="result%d" % mt)
-            (nc.gpsimd if mt < 2 else nc.vector).tensor_tensor(result[:], best[:], avail_sb[mt][:], ALU.mult)
+            (nc.gpsimd if mt < 0 else nc.vector).tensor_tensor(result[:], best[:], avail_sb[mt][:], ALU.mult)
             nc.sync.dma_start(out[P * mt : P * (mt + 1), :], result[:])

@@ -22,8 +22,12 @@ PACK = 4
 KP = P * PACK
 PASSES = 2
 TILES = S // P
-SCALAR_COLS = 368
-SCALAR_COLS_LAST = 176
+QUADRANTS = 4
+
+SCALAR_COLUMNS_FIRST, SCALAR_COLUMNS_MIDDLE, SCALAR_COLUMNS_LAST = 0, 448, 128
+
+RAW_BUFFERS = 6
+RING_BUFFERS = 3
 
 
 def tile_list_staffing_team_scores_kernel(
@@ -33,77 +37,65 @@ def tile_list_staffing_team_scores_kernel(
     nc = tc.nc
     with ExitStack() as ctx:
         keep = ctx.enter_context(tc.tile_pool(name="keep", bufs=1))
-        ring = ctx.enter_context(tc.tile_pool(name="ring", bufs=3))
+        ring = ctx.enter_context(tc.tile_pool(name="ring", bufs=RING_BUFFERS))
         psum = ctx.enter_context(tc.psum_pool(name="psum", bufs=1))
 
         def load_list(name, src):
-            t = keep.tile([P, S // 16], U16, name=name)
-            nc.sync.dma_start(t[:], src)
-            return t
+            offsets = keep.tile([P, S // 16], U16, name=name)
+            nc.sync.dma_start(offsets[:], src)
+            return offsets
 
-        def load_words(name, src, a, queue):
-            t = keep.tile([P, T], I32, name=name, align_bytes=64)
-            queue.dma_start(t[:], src[a].rearrange("p t i -> p (t i)").bitcast(I32))
-            return t
+        def load_words(name, src, a):
+            words = keep.tile([P, T], I32, name=name, align_bytes=64)
+            nc.sync.dma_start(words[:], src[a].rearrange("p t i -> p (t i)").bitcast(I32))
+            return words
 
         def zeroed_scale_tile(name, cols, engine):
-            t = keep.tile([P, cols], U8, name=name, align_bytes=64)
-            engine.memset(t[:].bitcast(I32), 0)
-            return t
+            plane = keep.tile([P, cols], U8, name=name, align_bytes=64)
+            engine.memset(plane[:].bitcast(I32), 0)
+            return plane
 
-        def load_side_by_side_quadrant(queue, t, src, q):
-            queue.dma_start(
-                t[32 * q : 32 * q + 4, :].bitcast(I32).rearrange("p (a w) -> p a w", a=PASSES),
-                src.bitcast(I32)[:, 4 * q : 4 * q + 4, :].rearrange("a r w -> r a w"),
-            )
+        def load_side_by_side_scales(planes, src):
+            for q in range(QUADRANTS):
+                nc.sync.dma_start(
+                    planes[32 * q : 32 * q + 4, :].bitcast(I32).rearrange("p (a w) -> p a w", a=PASSES),
+                    src.bitcast(I32)[:, 4 * q : 4 * q + 4, :].rearrange("a r w -> r a w"),
+                )
 
-        def load_stacked_quadrant(queue, t, src, q):
-            queue.dma_start(
-                t[32 * q : 32 * q + 8, :].bitcast(I32),
-                src.bitcast(I32)[:, 4 * q : 4 * q + 4, :],
-            )
+        def load_stacked_scales(planes, src):
+            for q in range(QUADRANTS):
+                nc.sync.dma_start(
+                    planes[32 * q : 32 * q + 8, :].bitcast(I32),
+                    src.bitcast(I32)[:, 4 * q : 4 * q + 4, :],
+                )
 
         def load_weight(name, w, a, b):
-            t = ring.tile([P, PACK, KP], F32, name=name, tag="w_raw", bufs=6, align_bytes=64)
+            raw = ring.tile([P, PACK, KP], F32, name=name, tag="w_raw", bufs=RAW_BUFFERS, align_bytes=64)
             nc.sync.dma_start(
-                t[:], w[KP * a : KP * (a + 1), KP * b : KP * (b + 1)].rearrange("(p i) c -> p i c", i=PACK)
+                raw[:], w[KP * a : KP * (a + 1), KP * b : KP * (b + 1)].rearrange("(p i) c -> p i c", i=PACK)
             )
-            return t
+            return raw
 
-        def gather_words(name, words, lst, pieces=1):
-            g = keep.tile([P, S], U32, name=name, align_bytes=64)
+        def gather_words(name, words, offsets, pieces=1):
+            picked = keep.tile([P, S], U32, name=name, align_bytes=64)
             n = S // pieces
             for u in range(pieces):
                 nc.vector.tensor_copy(
-                    g[:, n * u : n * (u + 1)],
-                    words[:].bitcast(U32).indirect(lst[:, n // 16 * u : n // 16 * (u + 1)]),
+                    picked[:, n * u : n * (u + 1)],
+                    words[:].bitcast(U32).indirect(offsets[:, n // 16 * u : n // 16 * (u + 1)]),
                 )
-            return g
+            return picked
 
-        def gather_bytes(name, window, lst):
-            g = keep.tile([P, S], U8, name=name, align_bytes=64)
-            nc.vector.tensor_copy(g[:], window.indirect(lst[:]))
-            return g
+        def gather_scales(name, window, offsets):
+            picked = keep.tile([P, S], U8, name=name, align_bytes=64)
+            nc.vector.tensor_copy(picked[:], window.indirect(offsets[:]))
+            return picked
 
         def by_neighbours(grouped, raw, cols):
             return (
                 grouped[:, cols, :].rearrange("p (c e) i -> p c i e", e=4),
                 raw[:, :, cols].rearrange("p i (c e) -> p c i e", e=4),
             )
-
-        def round_on_vector(grouped, raw, cols):
-            nc.vector.tensor_copy(*by_neighbours(grouped, raw, cols))
-
-        def round_on_gpsimd(grouped, raw, cols):
-            nc.gpsimd.tensor_scalar(
-                grouped[:, cols, :], raw[:, :, cols].rearrange("p i c -> p c i"), 1.0, 0.0, ALU.mult, ALU.add
-            )
-
-        def round_weight(raw, scalar_cols, round_rest):
-            g = ring.tile([P, KP, PACK], BF16, name="w_bf16", align_bytes=64)
-            nc.scalar.activation(*by_neighbours(g, raw, slice(0, scalar_cols)), ACT.Copy)
-            round_rest(g, raw, slice(scalar_cols, KP))
-            return g
 
         def quantise(name, grouped):
             codes = keep.tile([P, KP], U32, name=name + "_codes", align_bytes=64)
@@ -113,98 +105,110 @@ def tile_list_staffing_team_scores_kernel(
             )
             return codes, scales
 
-        v_scale_rows = zeroed_scale_tile("v_scale_rows", PASSES * T, nc.gpsimd)
-        w2_scale = zeroed_scale_tile("w2_scale", PASSES * H, nc.gpsimd)
-        v2_scale_rows = zeroed_scale_tile("v2_scale_rows", T, nc.vector)
-        v3_scale_rows = zeroed_scale_tile("v3_scale_rows", T, nc.vector)
-
-        for q in range(4):
-            load_side_by_side_quadrant(nc.scalar, v_scale_rows, tab_scales, q)
-        for q in range(4):
-            load_side_by_side_quadrant(nc.scalar, w2_scale, w2_scales, q)
-        for q in range(4):
-            load_stacked_quadrant(nc.gpsimd, v2_scale_rows, tab2_scales, q)
-        for q in range(4):
-            load_stacked_quadrant(nc.gpsimd, v3_scale_rows, tab3_scales, q)
-        identity = keep.tile([P, P], F32, name="identity")
-        make_identity(nc, identity[:])
-        gain_sb = keep.tile([P, PASSES, PACK], F32, name="gain_sb")
-        nc.gpsimd.dma_start(gain_sb[:], gain.rearrange("(b p i) -> p b i", b=PASSES, i=PACK))
-        v_words = []
-
-        idx = load_list("idx", offs)
-        raw = {}
-        v_words.append(load_words("v_words0", tab_words, 0, nc.sync))
-        w2_codes = keep.tile([P, PASSES, 2 * H], U8, name="w2_codes", align_bytes=64)
-        nc.sync.dma_start(w2_codes[:].bitcast(I32), w2_words.bitcast(I32).rearrange("a p w -> p a w"))
-        v_words.append(load_words("v_words1", tab_words, 1, nc.sync))
-        idx2 = load_list("idx2", offs2)
-        raw[1, 0, 0] = load_weight("w1_00", w1, 0, 0)
-        raw[1, 1, 0] = load_weight("w1_10", w1, 1, 0)
-        raw[1, 0, 1] = load_weight("w1_01", w1, 0, 1)
-        idx3 = load_list("idx3", offs3)
-        raw[1, 1, 1] = load_weight("w1_11", w1, 1, 1)
-        raw[3, 0, 0] = load_weight("w3_00", w3, 0, 0)
-        raw[3, 1, 0] = load_weight("w3_10", w3, 1, 0)
-        raw[3, 0, 1] = load_weight("w3_01", w3, 0, 1)
-        raw[3, 1, 1] = load_weight("w3_11", w3, 1, 1)
-        v2_words = [load_words("v2_words%d" % b, tab2_words, b, nc.sync) for b in range(PASSES)]
-        v3_words = [load_words("v3_words%d" % b, tab3_words, b, nc.sync) for b in range(PASSES)]
-        avail_sb = []
-        for mt in range(TILES):
-            t = keep.tile([P, S], F32, name="avail%d" % mt)
-            nc.sync.dma_start(t[:], avail[P * mt : P * (mt + 1), :])
-            avail_sb.append(t)
+        def round_and_quantise(name, raw, scalar_cols):
+            grouped = ring.tile([P, KP, PACK], BF16, name="w_bf16", align_bytes=64)
+            if scalar_cols > 0:
+                nc.scalar.activation(*by_neighbours(grouped, raw, slice(0, scalar_cols)), ACT.Copy)
+            nc.vector.tensor_copy(*by_neighbours(grouped, raw, slice(scalar_cols, KP)))
+            return quantise(name, grouped)
 
         def bank(n):
             return psum.tile([P, KP], F32, name="bank%d" % n)
 
-        def by_byte(bank):
-            return bank[:].rearrange("j (p i) -> j i p", i=PACK)
+        def by_byte(acc):
+            return acc[:].rearrange("j (p i) -> j i p", i=PACK)
 
-        wq = {}
-        v = []
+        v_scale_rows = zeroed_scale_tile("v_scale_rows", PASSES * T, nc.gpsimd)
+        w2_scale = zeroed_scale_tile("w2_scale", PASSES * H, nc.gpsimd)
+        v2_scale_rows = zeroed_scale_tile("v2_scale_rows", T, nc.vector)
+        v3_scale_rows = zeroed_scale_tile("v3_scale_rows", T, nc.vector)
+        identity = keep.tile([P, P], F32, name="identity")
+        make_identity(nc, identity[:])
 
-        def product(bank, jt, moving):
+        raw = {}
+        idx = load_list("idx", offs)
+        v_words = [load_words("v_words0", tab_words, 0)]
+        load_side_by_side_scales(v_scale_rows, tab_scales)
+        w2_codes = keep.tile([P, PASSES, 2 * H], U8, name="w2_codes", align_bytes=64)
+        nc.sync.dma_start(w2_codes[:].bitcast(I32), w2_words.bitcast(I32).rearrange("a p w -> p a w"))
+        load_side_by_side_scales(w2_scale, w2_scales)
+        v_words.append(load_words("v_words1", tab_words, 1))
+        load_stacked_scales(v2_scale_rows, tab2_scales)
+        idx2 = load_list("idx2", offs2)
+        raw["w1", 0, 0] = load_weight("w1_00", w1, 0, 0)
+        load_stacked_scales(v3_scale_rows, tab3_scales)
+        raw["w1", 1, 0] = load_weight("w1_10", w1, 1, 0)
+        raw["w1", 0, 1] = load_weight("w1_01", w1, 0, 1)
+        idx3 = load_list("idx3", offs3)
+        gain_sb = keep.tile([P, PASSES, PACK], F32, name="gain_sb")
+        nc.sync.dma_start(gain_sb[:], gain.rearrange("(b p i) -> p b i", b=PASSES, i=PACK))
+        raw["w1", 1, 1] = load_weight("w1_11", w1, 1, 1)
+        for b in range(PASSES):
+            for a in range(PASSES):
+                raw["w3", a, b] = load_weight("w3_%d%d" % (a, b), w3, a, b)
+        v2_words = [load_words("v2_words%d" % b, tab2_words, b) for b in range(PASSES)]
+        v3_words = [load_words("v3_words%d" % b, tab3_words, b) for b in range(PASSES)]
+        avail_sb = []
+        for mt in range(TILES):
+            rows = keep.tile([P, S], F32, name="avail%d" % mt)
+            nc.sync.dma_start(rows[:], avail[P * mt : P * (mt + 1), :])
+            avail_sb.append(rows)
+
+        v = [gather_words("v0", v_words[0], idx)]
+        v_scale = [gather_scales("v_scale%d" % a, v_scale_rows[:, T * a : T * (a + 1)], idx) for a in range(PASSES)]
+        v.append(gather_words("v1", v_words[1], idx))
+
+        quantised = {}
+        for n, (name, a, b) in enumerate(raw):
+            if n < PASSES:
+                scalar_cols = SCALAR_COLUMNS_FIRST
+            elif n < len(raw) - 1:
+                scalar_cols = SCALAR_COLUMNS_MIDDLE
+            else:
+                scalar_cols = SCALAR_COLUMNS_LAST
+            quantised[name, a, b] = round_and_quantise("%s_%d%d" % (name, a, b), raw[name, a, b], scalar_cols)
+
+        def first_stage_product(acc, jt, moving):
             cols = slice(P * jt, P * (jt + 1))
             for a in range(PASSES):
                 codes, scales = moving(a)
                 nc.tensor.matmul_mx(
-                    out=bank[:], lhsT=v[a][:, cols].bitcast(FP8X4), lhsT_scale=v_scale[a][:, cols],
+                    out=acc[:], lhsT=v[a][:, cols].bitcast(FP8X4), lhsT_scale=v_scale[a][:, cols],
                     rhs=codes, rhs_scale=scales, start=(a == 0), stop=(a == PASSES - 1),
                 )
 
-        def quantised_weight(which, b):
-            return lambda a: (wq[which, a, b][0][:].bitcast(FP8X4), wq[which, a, b][1][:])
+        def quantised_weight(name, b):
+            return lambda a: (quantised[name, a, b][0][:].bitcast(FP8X4), quantised[name, a, b][1][:])
 
-        def packed_weight(b):
+        def packed_w2(b):
             return lambda a: (
                 w2_codes[:, a, 2 * KP * b : 2 * KP * (b + 1)].bitcast(FP4X4),
                 w2_scale[:, H * a + KP * b : H * a + KP * (b + 1)],
             )
 
-        def d2_to_sbuf(b, jt):
-            d2 = bank(jt)
-            product(d2, jt, packed_weight(b))
-            d2_sb = keep.tile([P, PACK, P], F32, name="larger%d%d" % (b, jt), tag="larger%d%d" % (b, jt))
-            nc.scalar.activation(d2_sb[:], by_byte(d2), ACT.Copy)
-            return d2_sb
+        larger = {}
+        for b in range(PASSES):
+            for jt in range(TILES):
+                d2 = bank(jt)
+                first_stage_product(d2, jt, packed_w2(b))
+                larger[b, jt] = keep.tile([P, PACK, P], F32, name="larger%d%d" % (b, jt), tag="larger%d%d" % (b, jt))
+                nc.scalar.activation(larger[b, jt][:], by_byte(d2), ACT.Copy)
+        for b in range(PASSES):
+            for jt in range(TILES):
+                d1 = bank(TILES + jt)
+                first_stage_product(d1, jt, quantised_weight("w1", b))
+                nc.vector.tensor_tensor(larger[b, jt][:], by_byte(d1), larger[b, jt][:], ALU.max)
 
-        def larger_with_d1(b, jt, larger):
-            d1 = bank(4 + jt)
-            product(d1, jt, quantised_weight(1, b))
-            nc.vector.tensor_tensor(larger[:], by_byte(d1), larger[:], ALU.max)
+        def tanh_of_d3(b, jt):
+            d3 = bank(jt)
+            first_stage_product(d3, jt, quantised_weight("w3", b))
+            squashed = ring.tile([P, PACK, P], F32, name="squashed", bufs=TILES)
+            nc.scalar.activation(squashed[:], by_byte(d3), ACT.Tanh)
+            return squashed
 
-        def tanh_of_d3(b, jt, n):
-            d3 = bank(n)
-            product(d3, jt, quantised_weight(3, b))
-            th = ring.tile([P, PACK, P], F32, name="tanh_sb", bufs=4)
-            nc.scalar.activation(th[:], by_byte(d3), ACT.Tanh)
-            return th
-
-        def turn_and_round(b, jt, n, first, second, h_bf16):
-            total = bank(n)
-            for term, opens in ((first, True), (second, False)):
+        def add_turn_and_round(b, jt, squashed, h_bf16):
+            total = bank(TILES + jt)
+            for term, opens in ((larger[b, jt], True), (squashed, False)):
                 for i in range(PACK):
                     nc.tensor.matmul(
                         total[:, P * i : P * (i + 1)], term[:, i, :], identity[:],
@@ -217,48 +221,26 @@ def tile_list_staffing_team_scores_kernel(
                 ALU.mult,
             )
 
-        def prepare_weight(which, a, b, scalar_cols, round_rest):
-            g = round_weight(raw[which, a, b], scalar_cols, round_rest)
-            wq[which, a, b] = quantise("w%d_%d%d" % (which, a, b), g)
-
-        def second_half(b, larger, d3_banks, total_banks):
+        h = []
+        for b in range(PASSES):
             h_bf16 = keep.tile([P, S, PACK], BF16, name="h_bf16_%d" % b, align_bytes=64)
-            th = [tanh_of_d3(b, 0, d3_banks[0])]
+            squashed = [tanh_of_d3(b, 0)]
             for jt in range(TILES):
                 if jt + 1 < TILES:
-                    th.append(tanh_of_d3(b, jt + 1, d3_banks[jt + 1]))
-                turn_and_round(b, jt, total_banks[jt], larger[jt], th[jt], h_bf16)
-            return quantise("h%d" % b, h_bf16)
+                    squashed.append(tanh_of_d3(b, jt + 1))
+                add_turn_and_round(b, jt, squashed[jt], h_bf16)
+            h.append(quantise("h%d" % b, h_bf16))
 
-        v.append(gather_words("v0", v_words[0], idx))
-        v_scale = [gather_bytes("v_scale%d" % a, v_scale_rows[:, T * a : T * (a + 1)], idx) for a in range(PASSES)]
-        v.append(gather_words("v1", v_words[1], idx))
-        prepare_weight(1, 0, 0, 256, round_on_vector)
-        prepare_weight(1, 1, 0, 256, round_on_vector)
-        prepare_weight(1, 0, 1, 256, round_on_vector)
-        prepare_weight(1, 1, 1, 256, round_on_vector)
-        prepare_weight(3, 0, 0, 256, round_on_vector)
-        prepare_weight(3, 1, 0, 256, round_on_vector)
-        prepare_weight(3, 0, 1, 256, round_on_vector)
-        prepare_weight(3, 1, 1, 192, round_on_vector)
-        larger0 = [d2_to_sbuf(0, jt) for jt in range(TILES)]
-        larger1 = [d2_to_sbuf(1, jt) for jt in range(TILES)]
-        for jt in range(TILES):
-            larger_with_d1(0, jt, larger0[jt])
-        for jt in range(TILES):
-            larger_with_d1(1, jt, larger1[jt])
-        hq = [second_half(0, larger0, (0, 1, 2, 3), (4, 5, 6, 7))]
-        hq.append(second_half(1, larger1, (0, 1, 2, 3), (4, 5, 6, 7)))
-        v2_scale = gather_bytes("v2_scale", v2_scale_rows[:], idx2)
-        v3_scale = gather_bytes("v3_scale", v3_scale_rows[:], idx3)
+        v2_scale = gather_scales("v2_scale", v2_scale_rows[:], idx2)
+        v3_scale = gather_scales("v3_scale", v3_scale_rows[:], idx3)
         v2 = [gather_words("v2_%d" % b, v2_words[b], idx2) for b in range(PASSES)]
         v3 = [gather_words("v3_0", v3_words[0], idx3)]
 
-        def score_pass(acc, cand, cand_scale, mt, b, opens):
+        def score_pass(acc, candidates, candidate_scale, mt, b, opens):
             cols = slice(P * mt, P * (mt + 1))
             nc.tensor.matmul_mx(
-                out=acc[:], lhsT=cand[b][:, cols].bitcast(FP8X4), lhsT_scale=cand_scale[4 * b : P, cols],
-                rhs=hq[b][0][:].bitcast(FP8X4), rhs_scale=hq[b][1][:], start=opens, stop=not opens,
+                out=acc[:], lhsT=candidates[b][:, cols].bitcast(FP8X4), lhsT_scale=candidate_scale[4 * b : P, cols],
+                rhs=h[b][0][:].bitcast(FP8X4), rhs_scale=h[b][1][:], start=opens, stop=not opens,
             )
 
         e2_sb = []
@@ -266,16 +248,17 @@ def tile_list_staffing_team_scores_kernel(
             e2 = bank(mt)
             for b in range(PASSES):
                 score_pass(e2, v2, v2_scale, mt, b, b == 0)
-            t = keep.tile([P, S], F32, name="e2_sb%d" % mt, tag="larger0%d" % mt)
-            nc.scalar.activation(t[:], e2[:], ACT.Copy)
-            e2_sb.append(t)
-        v3.append(gather_words("v3_1", v3_words[1], idx3, pieces=4))
+            scores = keep.tile([P, S], F32, name="e2_sb%d" % mt, tag="larger0%d" % mt)
+            nc.scalar.activation(scores[:], e2[:], ACT.Copy)
+            e2_sb.append(scores)
+
+        v3.append(gather_words("v3_1", v3_words[1], idx3, pieces=TILES))
         for mt in range(TILES):
-            e3 = bank(4 + mt)
+            e3 = bank(TILES + mt)
             for b in (1, 0):
                 score_pass(e3, v3, v3_scale, mt, b, b == 1)
-            best = ring.tile([P, S], F32, name="best", bufs=4)
+            best = ring.tile([P, S], F32, name="best", bufs=TILES)
             nc.vector.tensor_tensor(best[:], e3[:], e2_sb[mt][:], ALU.max)
             result = keep.tile([P, S], F32, name="result%d" % mt)
-            (nc.gpsimd if mt < 0 else nc.vector).tensor_tensor(result[:], best[:], avail_sb[mt][:], ALU.mult)
+            nc.vector.tensor_tensor(result[:], best[:], avail_sb[mt][:], ALU.mult)
             nc.sync.dma_start(out[P * mt : P * (mt + 1), :], result[:])

from contextlib import ExitStack

import concourse.mybir as mybir
from concourse.masks import make_identity

K, H, T, S = 1024, 1024, 2048, 512
FLOPS = 2 * K * H * S * 3 + 2 * H * S * S * 2

F32 = mybir.dt.float32
BF16 = mybir.dt.bfloat16
I32 = mybir.dt.int32
U32 = mybir.dt.uint32
U16 = mybir.dt.uint16
U8 = mybir.dt.uint8
FP8X4 = mybir.dt.float8_e4m3fn_x4
FP4X4 = mybir.dt.float4_e2m1fn_x4
ACT = mybir.ActivationFunctionType
ALU = mybir.AluOpType

P = 128
PACK = 4
KP = P * PACK
PASSES = 2
TILES = S // P
QUADRANTS = 4

SCALAR_COLUMNS_FIRST, SCALAR_COLUMNS_MIDDLE, SCALAR_COLUMNS_LAST = 0, 448, 128

RAW_BUFFERS = 6
RING_BUFFERS = 3


def tile_list_staffing_team_scores_kernel(
    tc, tab_words, tab_scales, tab2_words, tab2_scales, tab3_words, tab3_scales,
    offs, offs2, offs3, w1, w2_words, w2_scales, w3, gain, avail, out,
):
    nc = tc.nc
    with ExitStack() as ctx:
        keep = ctx.enter_context(tc.tile_pool(name="keep", bufs=1))
        ring = ctx.enter_context(tc.tile_pool(name="ring", bufs=RING_BUFFERS))
        psum = ctx.enter_context(tc.psum_pool(name="psum", bufs=1))

        def load_list(name, src):
            offsets = keep.tile([P, S // 16], U16, name=name)
            nc.sync.dma_start(offsets[:], src)
            return offsets

        def load_words(name, src, a):
            words = keep.tile([P, T], I32, name=name, align_bytes=64)
            nc.sync.dma_start(words[:], src[a].rearrange("p t i -> p (t i)").bitcast(I32))
            return words

        def zeroed_scale_tile(name, cols, engine):
            plane = keep.tile([P, cols], U8, name=name, align_bytes=64)
            engine.memset(plane[:].bitcast(I32), 0)
            return plane

        def load_side_by_side_scales(planes, src):
            for q in range(QUADRANTS):
                nc.sync.dma_start(
                    planes[32 * q : 32 * q + 4, :].bitcast(I32).rearrange("p (a w) -> p a w", a=PASSES),
                    src.bitcast(I32)[:, 4 * q : 4 * q + 4, :].rearrange("a r w -> r a w"),
                )

        def load_stacked_scales(planes, src):
            for q in range(QUADRANTS):
                nc.sync.dma_start(
                    planes[32 * q : 32 * q + 8, :].bitcast(I32),
                    src.bitcast(I32)[:, 4 * q : 4 * q + 4, :],
                )

        def load_weight(name, w, a, b):
            raw = ring.tile([P, PACK, KP], F32, name=name, tag="w_raw", bufs=RAW_BUFFERS, align_bytes=64)
            nc.sync.dma_start(
                raw[:], w[KP * a : KP * (a + 1), KP * b : KP * (b + 1)].rearrange("(p i) c -> p i c", i=PACK)
            )
            return raw

        def gather_words(name, words, offsets, pieces=1):
            picked = keep.tile([P, S], U32, name=name, align_bytes=64)
            n = S // pieces
            for u in range(pieces):
                nc.vector.tensor_copy(
                    picked[:, n * u : n * (u + 1)],
                    words[:].bitcast(U32).indirect(offsets[:, n // 16 * u : n // 16 * (u + 1)]),
                )
            return picked

        def gather_scales(name, window, offsets):
            picked = keep.tile([P, S], U8, name=name, align_bytes=64)
            nc.vector.tensor_copy(picked[:], window.indirect(offsets[:]))
            return picked

        def by_neighbours(grouped, raw, cols):
            return (
                grouped[:, cols, :].rearrange("p (c e) i -> p c i e", e=4),
                raw[:, :, cols].rearrange("p i (c e) -> p c i e", e=4),
            )

        def quantise(name, grouped):
            codes = keep.tile([P, KP], U32, name=name + "_codes", align_bytes=64)
            scales = keep.tile([P, KP], U8, name=name + "_scales", align_bytes=64)
            nc.vector.quantize_mx(
                out=codes[:].bitcast(FP8X4), scales=scales[:], in_=grouped[:].rearrange("p c i -> p (c i)")
            )
            return codes, scales

        def round_and_quantise(name, raw, scalar_cols):
            grouped = ring.tile([P, KP, PACK], BF16, name="w_bf16", align_bytes=64)
            if scalar_cols > 0:
                nc.scalar.activation(*by_neighbours(grouped, raw, slice(0, scalar_cols)), ACT.Copy)
            nc.vector.tensor_copy(*by_neighbours(grouped, raw, slice(scalar_cols, KP)))
            return quantise(name, grouped)

        def bank(n):
            return psum.tile([P, KP], F32, name="bank%d" % n)

        def by_byte(acc):
            return acc[:].rearrange("j (p i) -> j i p", i=PACK)

        v_scale_rows = zeroed_scale_tile("v_scale_rows", PASSES * T, nc.gpsimd)
        w2_scale = zeroed_scale_tile("w2_scale", PASSES * H, nc.gpsimd)
        v2_scale_rows = zeroed_scale_tile("v2_scale_rows", T, nc.vector)
        v3_scale_rows = zeroed_scale_tile("v3_scale_rows", T, nc.vector)
        identity = keep.tile([P, P], F32, name="identity")
        make_identity(nc, identity[:])

        raw = {}
        idx = load_list("idx", offs)
        v_words = [load_words("v_words0", tab_words, 0)]
        load_side_by_side_scales(v_scale_rows, tab_scales)
        w2_codes = keep.tile([P, PASSES, 2 * H], U8, name="w2_codes", align_bytes=64)
        nc.sync.dma_start(w2_codes[:].bitcast(I32), w2_words.bitcast(I32).rearrange("a p w -> p a w"))
        load_side_by_side_scales(w2_scale, w2_scales)
        v_words.append(load_words("v_words1", tab_words, 1))
        load_stacked_scales(v2_scale_rows, tab2_scales)
        idx2 = load_list("idx2", offs2)
        raw["w1", 0, 0] = load_weight("w1_00", w1, 0, 0)
        load_stacked_scales(v3_scale_rows, tab3_scales)
        raw["w1", 1, 0] = load_weight("w1_10", w1, 1, 0)
        raw["w1", 0, 1] = load_weight("w1_01", w1, 0, 1)
        idx3 = load_list("idx3", offs3)
        gain_sb = keep.tile([P, PASSES, PACK], F32, name="gain_sb")
        nc.sync.dma_start(gain_sb[:], gain.rearrange("(b p i) -> p b i", b=PASSES, i=PACK))
        raw["w1", 1, 1] = load_weight("w1_11", w1, 1, 1)
        for b in range(PASSES):
            for a in range(PASSES):
                raw["w3", a, b] = load_weight("w3_%d%d" % (a, b), w3, a, b)
        v2_words = [load_words("v2_words%d" % b, tab2_words, b) for b in range(PASSES)]
        v3_words = [load_words("v3_words%d" % b, tab3_words, b) for b in range(PASSES)]
        avail_sb = []
        for mt in range(TILES):
            rows = keep.tile([P, S], F32, name="avail%d" % mt)
            nc.sync.dma_start(rows[:], avail[P * mt : P * (mt + 1), :])
            avail_sb.append(rows)

        v = [gather_words("v0", v_words[0], idx)]
        v_scale = [gather_scales("v_scale%d" % a, v_scale_rows[:, T * a : T * (a + 1)], idx) for a in range(PASSES)]
        v.append(gather_words("v1", v_words[1], idx))

        quantised = {}
        for n, (name, a, b) in enumerate(raw):
            if n < PASSES:
                scalar_cols = SCALAR_COLUMNS_FIRST
            elif n < len(raw) - 1:
                scalar_cols = SCALAR_COLUMNS_MIDDLE
            else:
                scalar_cols = SCALAR_COLUMNS_LAST
            quantised[name, a, b] = round_and_quantise("%s_%d%d" % (name, a, b), raw[name, a, b], scalar_cols)

        def first_stage_product(acc, jt, moving):
            cols = slice(P * jt, P * (jt + 1))
            for a in range(PASSES):
                codes, scales = moving(a)
                nc.tensor.matmul_mx(
                    out=acc[:], lhsT=v[a][:, cols].bitcast(FP8X4), lhsT_scale=v_scale[a][:, cols],
                    rhs=codes, rhs_scale=scales, start=(a == 0), stop=(a == PASSES - 1),
                )

        def quantised_weight(name, b):
            return lambda a: (quantised[name, a, b][0][:].bitcast(FP8X4), quantised[name, a, b][1][:])

        def packed_w2(b):
            return lambda a: (
                w2_codes[:, a, 2 * KP * b : 2 * KP * (b + 1)].bitcast(FP4X4),
                w2_scale[:, H * a + KP * b : H * a + KP * (b + 1)],
            )

        larger = {}
        for b in range(PASSES):
            for jt in range(TILES):
                d2 = bank(jt)
                first_stage_product(d2, jt, packed_w2(b))
                larger[b, jt] = keep.tile([P, PACK, P], F32, name="larger%d%d" % (b, jt), tag="larger%d%d" % (b, jt))
                nc.scalar.activation(larger[b, jt][:], by_byte(d2), ACT.Copy)
        for b in range(PASSES):
            for jt in range(TILES):
                d1 = bank(TILES + jt)
                first_stage_product(d1, jt, quantised_weight("w1", b))
                nc.vector.tensor_tensor(larger[b, jt][:], by_byte(d1), larger[b, jt][:], ALU.max)

        def tanh_of_d3(b, jt):
            d3 = bank(jt)
            first_stage_product(d3, jt, quantised_weight("w3", b))
            squashed = ring.tile([P, PACK, P], F32, name="squashed", bufs=TILES)
            nc.scalar.activation(squashed[:], by_byte(d3), ACT.Tanh)
            return squashed

        def add_turn_and_round(b, jt, squashed, h_bf16):
            total = bank(TILES + jt)
            for term, opens in ((larger[b, jt], True), (squashed, False)):
                for i in range(PACK):
                    nc.tensor.matmul(
                        total[:, P * i : P * (i + 1)], term[:, i, :], identity[:],
                        start=(opens and i == 0), stop=(not opens and i == PACK - 1), is_transpose=True,
                    )
            nc.vector.tensor_tensor(
                h_bf16[:, P * jt : P * (jt + 1), :],
                total[:].rearrange("p (i j) -> p j i", i=PACK),
                gain_sb[:, b : b + 1, :].to_broadcast([P, P, PACK]),
                ALU.mult,
            )

        h = []
        for b in range(PASSES):
            h_bf16 = keep.tile([P, S, PACK], BF16, name="h_bf16_%d" % b, align_bytes=64)
            squashed = [tanh_of_d3(b, 0)]
            for jt in range(TILES):
                if jt + 1 < TILES:
                    squashed.append(tanh_of_d3(b, jt + 1))
                add_turn_and_round(b, jt, squashed[jt], h_bf16)
            h.append(quantise("h%d" % b, h_bf16))

        v2_scale = gather_scales("v2_scale", v2_scale_rows[:], idx2)
        v3_scale = gather_scales("v3_scale", v3_scale_rows[:], idx3)
        v2 = [gather_words("v2_%d" % b, v2_words[b], idx2) for b in range(PASSES)]
        v3 = [gather_words("v3_0", v3_words[0], idx3)]

        def score_pass(acc, candidates, candidate_scale, mt, b, opens):
            cols = slice(P * mt, P * (mt + 1))
            nc.tensor.matmul_mx(
                out=acc[:], lhsT=candidates[b][:, cols].bitcast(FP8X4), lhsT_scale=candidate_scale[4 * b : P, cols],
                rhs=h[b][0][:].bitcast(FP8X4), rhs_scale=h[b][1][:], start=opens, stop=not opens,
            )

        e2_sb = []
        for mt in range(TILES):
            e2 = bank(mt)
            for b in range(PASSES):
                score_pass(e2, v2, v2_scale, mt, b, b == 0)
            scores = keep.tile([P, S], F32, name="e2_sb%d" % mt, tag="larger0%d" % mt)
            nc.scalar.activation(scores[:], e2[:], ACT.Copy)
            e2_sb.append(scores)

        v3.append(gather_words("v3_1", v3_words[1], idx3, pieces=TILES))
        for mt in range(TILES):
            e3 = bank(TILES + mt)
            for b in (1, 0):
                score_pass(e3, v3, v3_scale, mt, b, b == 1)
            best = ring.tile([P, S], F32, name="best", bufs=TILES)
            nc.vector.tensor_tensor(best[:], e3[:], e2_sb[mt][:], ALU.max)
            result = keep.tile([P, S], F32, name="result%d" % mt)
            nc.vector.tensor_tensor(result[:], best[:], avail_sb[mt][:], ALU.mult)
            nc.sync.dma_start(out[P * mt : P * (mt + 1), :], result[:])
